import numpy as np
import ml_dtypes


def mxq(x, axis, fmt="e4m3"):
    dtype, down = {"e4m3": (ml_dtypes.float8_e4m3fn, 7), "e5m2": (ml_dtypes.float8_e5m2, 14)}[fmt]
    v = np.moveaxis(np.asarray(x, np.float32).astype(ml_dtypes.bfloat16).astype(np.float64), axis, -1)
    blocks = v.reshape(v.shape[:-1] + (-1, 32))
    amax = np.abs(blocks).max(-1, keepdims=True)
    byte = np.maximum(np.where(amax > 0, np.frexp(amax)[1] - 1 + 127, 0) - down, 1)
    scale = np.exp2(byte - 127.0)
    codes = (blocks / scale).astype(np.float32).astype(dtype).astype(np.float64)
    return np.moveaxis((codes * scale).reshape(v.shape), -1, axis)


WIDE = False


def mx_kscale(k):
    if not WIDE:
        return np.ones(k)
    levels = np.array([10, -10, 5, -5, 0])
    if k % 512:
        return np.exp2(np.random.permutation(np.resize(levels, k // 32))).repeat(32)
    a = np.empty((k // 512, 16))
    for p in range(k // 512):
        a[p, :8] = np.random.permutation(np.resize(levels, 8))
        for g in range(8):
            far = levels[np.abs(levels - a[p, g]) >= 10]
            a[p, g + 8] = far[np.random.randint(len(far))]
    return np.exp2(a.ravel()).repeat(32)


def f64(x):
    return np.asarray(x).astype(np.float64)


def striped(idx):
    return np.tile(np.asarray(idx).reshape(-1, 16).T, (8, 1)).astype(np.uint16)


def unstriped(offs):
    return offs[:16].T.reshape(-1).astype(np.int64)


E2M1 = np.array([0.0, 0.5, 1.0, 1.5, 2.0, 3.0, 4.0, 6.0, -0.0, -0.5, -1.0, -1.5, -2.0, -3.0, -4.0, -6.0])


def pack_weight(w, fmt):
    k, n = w.shape
    w = f64(np.asarray(w, np.float32).astype(ml_dtypes.bfloat16)).reshape(k // 32, 32, n)
    amax = np.abs(w).max(1)
    if fmt == "e4m3":
        byte = np.frexp(amax)[1] - 1 + 127 - 7
    else:
        mant, ex = np.frexp(amax / 6.0)
        byte = np.where(mant > 0.5, ex, ex - 1) + 127
    byte = np.clip(np.where(amax > 0, byte, 1), 1, 254)
    scaled = (w * np.exp2(127.0 - byte)[:, None, :]).reshape(k, n).astype(np.float32)
    by_word = np.ascontiguousarray(scaled.reshape(k // 512, 128, 4, n).transpose(0, 1, 3, 2))
    if fmt == "e4m3":
        words = by_word.astype(ml_dtypes.float8_e4m3fn).view(np.uint8)
    else:
        c = by_word.astype(ml_dtypes.float4_e2m1fn).view(np.uint8) & 0xF
        words = (c[..., 0::2] | (c[..., 1::2] << 4)).reshape(k // 512, 128, 2 * n)
    return np.ascontiguousarray(words), np.ascontiguousarray(byte.astype(np.uint8).reshape(k // 512, 16, n))


def unpack_weight(words, scales, fmt):
    g, _, n = scales.shape
    words = np.ascontiguousarray(words).reshape(g, 128, n, -1)
    if fmt == "e4m3":
        vals = words.view(ml_dtypes.float8_e4m3fn).astype(np.float64)
    else:
        nib = np.empty((g, 128, n, 4), np.uint8)
        nib[..., 0::2] = words & 0xF
        nib[..., 1::2] = words >> 4
        vals = E2M1[nib]
    vals = vals * np.repeat(np.exp2(scales.astype(np.float64) - 127.0), 8, axis=1)[..., None]
    return vals.transpose(0, 1, 3, 2).reshape(g * 512, n)


K, T, J, I, N = 1024, 1024, 512, 512, 512


def setup_inputs():
    n = np.random.standard_normal
    idx = np.random.permutation(T)[:J]
    idx2 = np.random.permutation(T)[:I]
    fk = mx_kscale(K)
    fj = mx_kscale(J)
    xqp = pack_weight(n((K, T)) / fk[:, None], "e4m3")
    wap = pack_weight(n((K, N)) * 1 / np.sqrt(K) * fk[:, None], "e2m1")
    mixp = pack_weight(n((J, I)) * 1 / np.sqrt(J) * fj[:, None], "e4m3")
    return {
        "xq_words": xqp[0],
        "xq_scales": xqp[1],
        "wa_words": wap[0],
        "wa_scales": wap[1],
        "cj": (np.random.uniform(0.5, 2.0, (1, J)) / fj).astype(np.float32),
        "mix_words": mixp[0],
        "mix_scales": mixp[1],
        "res": (1.0 * n((N, T))).astype(np.float32),
        "offs": striped(idx),
        "offs2": striped(idx2),
    }


def reference(xq_words, xq_scales, wa_words, wa_scales, cj, mix_words, mix_scales, res, offs, offs2):
    idx = unstriped(offs)
    idx2 = unstriped(offs2)
    xqu = unpack_weight(xq_words, xq_scales, "e4m3")
    wau = unpack_weight(wa_words, wa_scales, "e2m1")
    mixu = unpack_weight(mix_words, mix_scales, "e4m3")
    xqidxg = xqu[:, idx]
    a = wau.T @ xqidxg
    aw = a * f64(cj)
    at = aw.T
    atq = mxq(at, 0, "e4m3")
    m = atq.T @ mixu
    mp = np.zeros((N, T))
    mp[:, idx2] = m
    y = 0.3 * f64(res) + mp
    return y

@@ -1,0 +1,178 @@
+from contextlib import ExitStack
+
+import concourse.mybir as mybir
+
+K, T, J, I, N = 1024, 1024, 512, 512, 512
+FLOPS = 2 * K * J * N + 2 * J * N * I
+
+F32 = mybir.dt.float32
+BF16 = mybir.dt.bfloat16
+I32 = mybir.dt.int32
+U32 = mybir.dt.uint32
+U16 = mybir.dt.uint16
+U8 = mybir.dt.uint8
+FP8X4 = mybir.dt.float8_e4m3fn_x4
+FP4X4 = mybir.dt.float4_e2m1fn_x4
+MULT = mybir.AluOpType.mult
+ADD = mybir.AluOpType.add
+COPY = mybir.ActivationFunctionType.Copy
+
+P = 128
+PACK = 4
+PASSES = K // (P * PACK)
+TILES = N // P
+QUADS = 4
+PER_COLUMN = 16
+RES_FACTOR = 0.3
+
+
+def tile_list_expert_slot_mixing_kernel(
+    tc, xq_words, xq_scales, wa_words, wa_scales, cj, mix_words, mix_scales, res, offs, offs2, out
+):
+    nc = tc.nc
+    with ExitStack() as ctx:
+        keep = ctx.enter_context(tc.tile_pool(name="keep", bufs=1))
+        early = ctx.enter_context(tc.tile_pool(name="early", bufs=1))
+        psum = ctx.enter_context(tc.psum_pool(name="psum", bufs=1))
+
+        def tile(shape, dtype, name, tag=None):
+            return keep.tile(shape, dtype, name=name, tag=tag or name, align_bytes=64)
+
+        picks = keep.tile([P, J // PER_COLUMN], U16, name="picks")
+        places = keep.tile([P, I // PER_COLUMN], U16, name="places")
+        factor = tile([P, PACK], F32, "factor")
+        x_scales = early.tile([P, T], U8, name="x_scales", align_bytes=64, offset=0)
+        x_words = [tile([P, T], I32, "x_words%d" % z, "x%d" % z) for z in range(PASSES)]
+        w_words = tile([P, PASSES, 2 * N], U8, "w_words", "w")
+        w_scales = tile([P, PASSES, N], U8, "w_scales")
+        moved_scales = tile([P, J], U8, "moved_scales")
+
+        nc.vector.memset(moved_scales[:].bitcast(I32), 0)
+        nc.gpsimd.memset(w_scales[:].bitcast(I32), 0)
+
+        nc.sync.dma_start(picks[:], offs)
+        nc.sync.dma_start(
+            out=x_scales[0:32, :].bitcast(I32), in_=xq_scales.rearrange("z q c -> (z q) c").bitcast(I32)
+        )
+        for q in range(1, QUADS):
+            nc.sync.dma_start(
+                out=x_scales[32 * q : 32 * (q + 1), :].bitcast(I32),
+                in_=xq_scales[0, 4 * q : 4 * q + 4, :].bitcast(I32).unsqueeze(0).to_broadcast([8, 4, T // 4]),
+            )
+        for z in range(PASSES):
+            nc.sync.dma_start(out=x_words[z][:], in_=xq_words[z].rearrange("p c r -> p (c r)").bitcast(I32))
+        nc.sync.dma_start(out=w_words[:].bitcast(I32), in_=wa_words.rearrange("z p c -> p z c").bitcast(I32))
+        nc.sync.dma_start(places[:], offs2)
+        nc.sync.dma_start(out=factor[:], in_=cj.rearrange("o (p t) -> p (o t)", t=PACK))
+        for q in range(QUADS):
+            nc.gpsimd.dma_start(
+                out=w_scales[32 * q : 32 * q + 4].bitcast(I32),
+                in_=wa_scales[:, 4 * q : 4 * q + 4, :].rearrange("z r n -> r z n").bitcast(I32),
+            )
+
+        got_scales = tile([P, PACK, P], U8, "got_scales")
+        nc.vector.tensor_copy(got_scales[:].rearrange("p t s -> p s t"), x_scales[:].indirect(picks[:]))
+        got_flat = got_scales[:].rearrange("p t s -> p (t s)")
+        for q in range(QUADS):
+            nc.scalar.dma_start(
+                out=moved_scales[32 * q : 32 * q + 4, :].bitcast(I32),
+                in_=got_flat[16 + 4 * q : 16 + 4 * q + 4, :].bitcast(I32),
+            )
+        got_words = []
+        for z in range(PASSES):
+            got = tile([P, PACK, P], U32, "got_words%d" % z, "got%d" % z)
+            nc.vector.tensor_copy(got[:].rearrange("p t s -> p s t"), x_words[z][:].bitcast(U32).indirect(picks[:]))
+            got_words.append(got)
+        slot_scales = [got_flat, moved_scales[:]]
+
+        mix_scale = early.tile([P, I], U8, name="mix_scale", align_bytes=64, offset=0)
+        mix = early.tile([P, I], I32, name="mix", align_bytes=64, offset=I)
+        nc.sync.dma_start(out=mix[:], in_=mix_words[0].rearrange("p c r -> p (c r)").bitcast(I32))
+        nc.vector.memset(mix_scale[:].bitcast(I32), 0)
+        for q in range(QUADS):
+            nc.sync.dma_start(
+                out=mix_scale[32 * q : 32 * q + 4, :].bitcast(I32),
+                in_=mix_scales[0, 4 * q : 4 * q + 4, :].bitcast(I32),
+            )
+
+        pages = [tile([P, T], F32, "page%d" % b, "x1" if b == 3 else None) for b in range(TILES)]
+
+        mixed = []
+        for b in range(TILES):
+            acc = psum.tile([P, PACK, P], F32, name="acc%d" % b)
+            for z in range(PASSES):
+                for t in range(PACK):
+                    nc.tensor.matmul_mx(
+                        out=acc[:, t, :],
+                        lhsT=got_words[z][:, t, :].bitcast(FP8X4),
+                        lhsT_scale=slot_scales[z][:, t * P : (t + 1) * P],
+                        rhs=w_words[:, z, 2 * P * b : 2 * P * (b + 1)].bitcast(FP4X4),
+                        rhs_scale=w_scales[:, z, P * b : P * (b + 1)],
+                        start=(z == 0 and t == 0),
+                        stop=(z == PASSES - 1 and t == PACK - 1),
+                    )
+            at = tile([P, P, PACK], BF16, "at%d" % b)
+            nc.vector.tensor_tensor(
+                at[:],
+                acc[:].rearrange("p t n -> p n t"),
+                factor[:].unsqueeze(1).to_broadcast([P, P, PACK]),
+                MULT,
+            )
+            at_codes = tile([P, P], U32, "at_codes%d" % b)
+            at_scales = tile([P, P], U8, "at_scales%d" % b)
+            nc.vector.quantize_mx(
+                out=at_codes[:].bitcast(FP8X4), scales=at_scales[:], in_=at[:].rearrange("p n t -> p (n t)")
+            )
+            bank = psum.tile([P, I], F32, name="mixed%d" % b)
+            nc.tensor.matmul_mx(
+                out=bank[:],
+                lhsT=at_codes[:].bitcast(FP8X4),
+                lhsT_scale=at_scales[:],
+                rhs=mix[:].bitcast(FP8X4),
+                rhs_scale=mix_scale[:],
+                start=True,
+                stop=True,
+            )
+            mixed.append(bank)
+
+        for page in pages:
+            nc.vector.memset(page[:], 0.0)
+
+        res_tags = ["x0", "got0", "got1", "w"]
+        rows = []
+        for b in range(TILES):
+            row = tile([P, T], F32, "res%d" % b, res_tags[b])
+            nc.sync.dma_start(out=row[:], in_=res[P * b : P * (b + 1), :])
+            rows.append(row)
+
+        values = [tile([P, I], F32, "m%d" % b) for b in range(TILES)]
+
+        def scatter(on_vector, b, first, last):
+            window = pages[b][:].indirect(places[:, first // PER_COLUMN : last // PER_COLUMN])
+            if on_vector:
+                nc.vector.tensor_copy(window, values[b][:, first:last])
+            else:
+                nc.scalar.activation(window, values[b][:, first:last], COPY)
+
+        nc.scalar.copy(values[0][:], mixed[0][:])
+        scatter(False, 0, 0, 256)
+        scatter(False, 0, 256, 512)
+        nc.vector.tensor_copy(values[1][:], mixed[1][:])
+        scatter(True, 1, 0, 512)
+        nc.scalar.copy(values[2][:], mixed[2][:])
+        scatter(False, 2, 0, 256)
+        scatter(False, 2, 256, 512)
+        nc.vector.tensor_copy(values[3][:], mixed[3][:])
+        scatter(True, 3, 0, 128)
+        scatter(False, 3, 128, 512)
+
+        for b in range(TILES):
+            result = tile([P, T], F32, "result%d" % b)
+            parts = 2 if b == TILES - 1 else 1
+            width = T // parts
+            for h in range(parts):
+                cols = slice(h * width, (h + 1) * width)
+                nc.vector.scalar_tensor_tensor(
+                    result[:, cols], rows[b][:, cols], RES_FACTOR, pages[b][:, cols], MULT, ADD
+                )
+                nc.sync.dma_start(out=out[P * b : P * (b + 1), cols], in_=result[:, cols])

@@ -24,6 +24,7 @@ TILES = N // P
 QUADS = 4
 PER_COLUMN = 16
 RES_FACTOR = 0.3
+SHARE = 128
 
 
 def tile_list_expert_slot_mixing_kernel(
@@ -40,16 +41,16 @@ def tile_list_expert_slot_mixing_kernel(
 
         picks = keep.tile([P, J // PER_COLUMN], U16, name="picks")
         places = keep.tile([P, I // PER_COLUMN], U16, name="places")
-        factor = tile([P, PACK], F32, "factor")
         x_scales = early.tile([P, T], U8, name="x_scales", align_bytes=64, offset=0)
         x_words = [tile([P, T], I32, "x_words%d" % z, "x%d" % z) for z in range(PASSES)]
-        w_words = tile([P, PASSES, 2 * N], U8, "w_words", "w")
         w_scales = tile([P, PASSES, N], U8, "w_scales")
         moved_scales = tile([P, J], U8, "moved_scales")
 
-        nc.vector.memset(moved_scales[:].bitcast(I32), 0)
-        nc.gpsimd.memset(w_scales[:].bitcast(I32), 0)
+        nc.vector.memset(w_scales[:].bitcast(I32), 0)
+        nc.gpsimd.memset(moved_scales[:].bitcast(I32), 0)
 
+        factor = tile([P, PACK], F32, "factor")
+        nc.gpsimd.dma_start(out=factor[:], in_=cj.rearrange("o (p t) -> p (o t)", t=PACK))
         nc.sync.dma_start(picks[:], offs)
         nc.sync.dma_start(
             out=x_scales[0:32, :].bitcast(I32), in_=xq_scales.rearrange("z q c -> (z q) c").bitcast(I32)
@@ -59,16 +60,16 @@ def tile_list_expert_slot_mixing_kernel(
                 out=x_scales[32 * q : 32 * (q + 1), :].bitcast(I32),
                 in_=xq_scales[0, 4 * q : 4 * q + 4, :].bitcast(I32).unsqueeze(0).to_broadcast([8, 4, T // 4]),
             )
-        for z in range(PASSES):
-            nc.sync.dma_start(out=x_words[z][:], in_=xq_words[z].rearrange("p c r -> p (c r)").bitcast(I32))
-        nc.sync.dma_start(out=w_words[:].bitcast(I32), in_=wa_words.rearrange("z p c -> p z c").bitcast(I32))
-        nc.sync.dma_start(places[:], offs2)
-        nc.sync.dma_start(out=factor[:], in_=cj.rearrange("o (p t) -> p (o t)", t=PACK))
+        nc.sync.dma_start(out=x_words[0][:], in_=xq_words[0].rearrange("p c r -> p (c r)").bitcast(I32))
         for q in range(QUADS):
-            nc.gpsimd.dma_start(
+            nc.sync.dma_start(
                 out=w_scales[32 * q : 32 * q + 4].bitcast(I32),
                 in_=wa_scales[:, 4 * q : 4 * q + 4, :].rearrange("z r n -> r z n").bitcast(I32),
             )
+        nc.sync.dma_start(out=x_words[1][:], in_=xq_words[1].rearrange("p c r -> p (c r)").bitcast(I32))
+        w_words = tile([P, PASSES, 2 * N], U8, "w_words")
+        nc.sync.dma_start(out=w_words[:].bitcast(I32), in_=wa_words.rearrange("z p c -> p z c").bitcast(I32))
+        nc.sync.dma_start(places[:], offs2)
 
         got_scales = tile([P, PACK, P], U8, "got_scales")
         nc.vector.tensor_copy(got_scales[:].rearrange("p t s -> p s t"), x_scales[:].indirect(picks[:]))
@@ -85,21 +86,18 @@ def tile_list_expert_slot_mixing_kernel(
             got_words.append(got)
         slot_scales = [got_flat, moved_scales[:]]
 
-        mix_scale = early.tile([P, I], U8, name="mix_scale", align_bytes=64, offset=0)
-        mix = early.tile([P, I], I32, name="mix", align_bytes=64, offset=I)
+        mix_scale = early.tile([P, I], U8, name="mix_scale", align_bytes=64, offset=64)
+        mix = early.tile([P, I], I32, name="mix", align_bytes=64, offset=576)
         nc.sync.dma_start(out=mix[:], in_=mix_words[0].rearrange("p c r -> p (c r)").bitcast(I32))
-        nc.vector.memset(mix_scale[:].bitcast(I32), 0)
+        nc.gpsimd.memset(mix_scale[:].bitcast(I32), 0)
         for q in range(QUADS):
             nc.sync.dma_start(
                 out=mix_scale[32 * q : 32 * q + 4, :].bitcast(I32),
                 in_=mix_scales[0, 4 * q : 4 * q + 4, :].bitcast(I32),
             )
 
-        pages = [tile([P, T], F32, "page%d" % b, "x1" if b == 3 else None) for b in range(TILES)]
-
-        mixed = []
-        for b in range(TILES):
-            acc = psum.tile([P, PACK, P], F32, name="acc%d" % b)
+        def quantised(b):
+            acc = psum.tile([P, PACK, P], F32, name="acc%d" % b, tag="bank%d" % b)
             for z in range(PASSES):
                 for t in range(PACK):
                     nc.tensor.matmul_mx(
@@ -123,51 +121,69 @@ def tile_list_expert_slot_mixing_kernel(
             nc.vector.quantize_mx(
                 out=at_codes[:].bitcast(FP8X4), scales=at_scales[:], in_=at[:].rearrange("p n t -> p (n t)")
             )
-            bank = psum.tile([P, I], F32, name="mixed%d" % b)
+            return at_codes, at_scales
+
+        def mixed(at, first, last, bank_tag):
+            bank = psum.tile([P, last - first], F32, name="mixed", tag=bank_tag)
             nc.tensor.matmul_mx(
                 out=bank[:],
-                lhsT=at_codes[:].bitcast(FP8X4),
-                lhsT_scale=at_scales[:],
-                rhs=mix[:].bitcast(FP8X4),
-                rhs_scale=mix_scale[:],
+                lhsT=at[0][:].bitcast(FP8X4),
+                lhsT_scale=at[1][:],
+                rhs=mix[:, first:last].bitcast(FP8X4),
+                rhs_scale=mix_scale[:, first:last],
                 start=True,
                 stop=True,
             )
-            mixed.append(bank)
+            return bank
 
-        for page in pages:
-            nc.vector.memset(page[:], 0.0)
+        def cleared(b, tag=None):
+            page = tile([P, T], F32, "page%d" % b, tag)
+            nc.vector.memset(page[:].bitcast(I32), 0)
+            return page
 
-        res_tags = ["x0", "got0", "got1", "w"]
+        def places_of(page, first, last):
+            return page[:].indirect(places[:, first // PER_COLUMN : last // PER_COLUMN])
+
+        half = I // 2
+        pages = [cleared(0), cleared(1), cleared(2, "x1")]
+
+        at0 = quantised(0)
+        for h in range(2):
+            bank = mixed(at0, h * half, (h + 1) * half, "bank%d" % (2 + h))
+            m = tile([P, half], F32, "m0_%d" % h)
+            nc.scalar.copy(m[:], bank[:])
+            nc.scalar.activation(places_of(pages[0], h * half, (h + 1) * half), m[:], COPY)
+
+        bank1 = mixed(quantised(1), 0, I, "bank4")
+        pages.append(cleared(3, "at1"))
+        bank2 = mixed(quantised(2), 0, I, "bank5")
+        m = tile([P, SHARE], F32, "m1_first")
+        nc.vector.tensor_copy(m[:], bank1[:, 0:SHARE])
+        nc.vector.tensor_copy(places_of(pages[1], 0, SHARE), m[:])
+        bank3 = mixed(quantised(3), 0, I, "bank6")
+        m = tile([P, I - SHARE], F32, "m1_rest", "at3")
+        nc.vector.tensor_copy(m[:], bank1[:, SHARE:I])
+        nc.vector.tensor_copy(places_of(pages[1], SHARE, I), m[:])
+
+        m = tile([P, I], F32, "m2")
+        nc.scalar.copy(m[:], bank2[:])
+        nc.scalar.activation(places_of(pages[2], 0, I - SHARE), m[:, 0 : I - SHARE], COPY)
+        nc.vector.tensor_copy(places_of(pages[2], I - SHARE, I), m[:, I - SHARE : I])
+
+        m = tile([P, I], F32, "m3")
+        nc.scalar.copy(m[:], bank3[:])
+        for h in range(2):
+            nc.scalar.activation(places_of(pages[3], h * half, (h + 1) * half), m[:, h * half : (h + 1) * half], COPY)
+
+        res_tags = ["x0", "got0", "got1", "w_words"]
         rows = []
         for b in range(TILES):
             row = tile([P, T], F32, "res%d" % b, res_tags[b])
             nc.sync.dma_start(out=row[:], in_=res[P * b : P * (b + 1), :])
             rows.append(row)
 
-        values = [tile([P, I], F32, "m%d" % b) for b in range(TILES)]
-
-        def scatter(on_vector, b, first, last):
-            window = pages[b][:].indirect(places[:, first // PER_COLUMN : last // PER_COLUMN])
-            if on_vector:
-                nc.vector.tensor_copy(window, values[b][:, first:last])
-            else:
-                nc.scalar.activation(window, values[b][:, first:last], COPY)
-
-        nc.scalar.copy(values[0][:], mixed[0][:])
-        scatter(False, 0, 0, 256)
-        scatter(False, 0, 256, 512)
-        nc.vector.tensor_copy(values[1][:], mixed[1][:])
-        scatter(True, 1, 0, 512)
-        nc.scalar.copy(values[2][:], mixed[2][:])
-        scatter(False, 2, 0, 256)
-        scatter(False, 2, 256, 512)
-        nc.vector.tensor_copy(values[3][:], mixed[3][:])
-        scatter(True, 3, 0, 128)
-        scatter(False, 3, 128, 512)
-
         for b in range(TILES):
-            result = tile([P, T], F32, "result%d" % b)
+            result = tile([P, T], F32, "result%d" % b, "at3" if b == 0 else None)
             parts = 2 if b == TILES - 1 else 1
             width = T // parts
             for h in range(parts):

from contextlib import ExitStack

import concourse.mybir as mybir

K, T, J, I, N = 1024, 1024, 512, 512, 512
FLOPS = 2 * K * J * N + 2 * J * N * I

F32 = mybir.dt.float32
BF16 = mybir.dt.bfloat16
I32 = mybir.dt.int32
U32 = mybir.dt.uint32
U16 = mybir.dt.uint16
U8 = mybir.dt.uint8
FP8X4 = mybir.dt.float8_e4m3fn_x4
FP4X4 = mybir.dt.float4_e2m1fn_x4
MULT = mybir.AluOpType.mult
ADD = mybir.AluOpType.add
COPY = mybir.ActivationFunctionType.Copy

P = 128
PACK = 4
PASSES = K // (P * PACK)
TILES = N // P
QUADS = 4
PER_COLUMN = 16
RES_FACTOR = 0.3
SHARE = 128


def tile_list_expert_slot_mixing_kernel(
    tc, xq_words, xq_scales, wa_words, wa_scales, cj, mix_words, mix_scales, res, offs, offs2, out
):
    nc = tc.nc
    with ExitStack() as ctx:
        keep = ctx.enter_context(tc.tile_pool(name="keep", bufs=1))
        early = ctx.enter_context(tc.tile_pool(name="early", bufs=1))
        psum = ctx.enter_context(tc.psum_pool(name="psum", bufs=1))

        def tile(shape, dtype, name, tag=None):
            return keep.tile(shape, dtype, name=name, tag=tag or name, align_bytes=64)

        picks = keep.tile([P, J // PER_COLUMN], U16, name="picks")
        places = keep.tile([P, I // PER_COLUMN], U16, name="places")
        x_scales = early.tile([P, T], U8, name="x_scales", align_bytes=64, offset=0)
        x_words = [tile([P, T], I32, "x_words%d" % z, "x%d" % z) for z in range(PASSES)]
        w_scales = tile([P, PASSES, N], U8, "w_scales")
        moved_scales = tile([P, J], U8, "moved_scales")

        nc.vector.memset(w_scales[:].bitcast(I32), 0)
        nc.gpsimd.memset(moved_scales[:].bitcast(I32), 0)

        factor = tile([P, PACK], F32, "factor")
        nc.gpsimd.dma_start(out=factor[:], in_=cj.rearrange("o (p t) -> p (o t)", t=PACK))
        nc.sync.dma_start(picks[:], offs)
        nc.sync.dma_start(
            out=x_scales[0:32, :].bitcast(I32), in_=xq_scales.rearrange("z q c -> (z q) c").bitcast(I32)
        )
        for q in range(1, QUADS):
            nc.sync.dma_start(
                out=x_scales[32 * q : 32 * (q + 1), :].bitcast(I32),
                in_=xq_scales[0, 4 * q : 4 * q + 4, :].bitcast(I32).unsqueeze(0).to_broadcast([8, 4, T // 4]),
            )
        nc.sync.dma_start(out=x_words[0][:], in_=xq_words[0].rearrange("p c r -> p (c r)").bitcast(I32))
        for q in range(QUADS):
            nc.sync.dma_start(
                out=w_scales[32 * q : 32 * q + 4].bitcast(I32),
                in_=wa_scales[:, 4 * q : 4 * q + 4, :].rearrange("z r n -> r z n").bitcast(I32),
            )
        nc.sync.dma_start(out=x_words[1][:], in_=xq_words[1].rearrange("p c r -> p (c r)").bitcast(I32))
        w_words = tile([P, PASSES, 2 * N], U8, "w_words")
        nc.sync.dma_start(out=w_words[:].bitcast(I32), in_=wa_words.rearrange("z p c -> p z c").bitcast(I32))
        nc.sync.dma_start(places[:], offs2)

        got_scales = tile([P, PACK, P], U8, "got_scales")
        nc.vector.tensor_copy(got_scales[:].rearrange("p t s -> p s t"), x_scales[:].indirect(picks[:]))
        got_flat = got_scales[:].rearrange("p t s -> p (t s)")
        for q in range(QUADS):
            nc.scalar.dma_start(
                out=moved_scales[32 * q : 32 * q + 4, :].bitcast(I32),
                in_=got_flat[16 + 4 * q : 16 + 4 * q + 4, :].bitcast(I32),
            )
        got_words = []
        for z in range(PASSES):
            got = tile([P, PACK, P], U32, "got_words%d" % z, "got%d" % z)
            nc.vector.tensor_copy(got[:].rearrange("p t s -> p s t"), x_words[z][:].bitcast(U32).indirect(picks[:]))
            got_words.append(got)
        slot_scales = [got_flat, moved_scales[:]]

        mix_scale = early.tile([P, I], U8, name="mix_scale", align_bytes=64, offset=64)
        mix = early.tile([P, I], I32, name="mix", align_bytes=64, offset=576)
        nc.sync.dma_start(out=mix[:], in_=mix_words[0].rearrange("p c r -> p (c r)").bitcast(I32))
        nc.gpsimd.memset(mix_scale[:].bitcast(I32), 0)
        for q in range(QUADS):
            nc.sync.dma_start(
                out=mix_scale[32 * q : 32 * q + 4, :].bitcast(I32),
                in_=mix_scales[0, 4 * q : 4 * q + 4, :].bitcast(I32),
            )

        def quantised(b):
            acc = psum.tile([P, PACK, P], F32, name="acc%d" % b, tag="bank%d" % b)
            for z in range(PASSES):
                for t in range(PACK):
                    nc.tensor.matmul_mx(
                        out=acc[:, t, :],
                        lhsT=got_words[z][:, t, :].bitcast(FP8X4),
                        lhsT_scale=slot_scales[z][:, t * P : (t + 1) * P],
                        rhs=w_words[:, z, 2 * P * b : 2 * P * (b + 1)].bitcast(FP4X4),
                        rhs_scale=w_scales[:, z, P * b : P * (b + 1)],
                        start=(z == 0 and t == 0),
                        stop=(z == PASSES - 1 and t == PACK - 1),
                    )
            at = tile([P, P, PACK], BF16, "at%d" % b)
            nc.vector.tensor_tensor(
                at[:],
                acc[:].rearrange("p t n -> p n t"),
                factor[:].unsqueeze(1).to_broadcast([P, P, PACK]),
                MULT,
            )
            at_codes = tile([P, P], U32, "at_codes%d" % b)
            at_scales = tile([P, P], U8, "at_scales%d" % b)
            nc.vector.quantize_mx(
                out=at_codes[:].bitcast(FP8X4), scales=at_scales[:], in_=at[:].rearrange("p n t -> p (n t)")
            )
            return at_codes, at_scales

        def mixed(at, first, last, bank_tag):
            bank = psum.tile([P, last - first], F32, name="mixed", tag=bank_tag)
            nc.tensor.matmul_mx(
                out=bank[:],
                lhsT=at[0][:].bitcast(FP8X4),
                lhsT_scale=at[1][:],
                rhs=mix[:, first:last].bitcast(FP8X4),
                rhs_scale=mix_scale[:, first:last],
                start=True,
                stop=True,
            )
            return bank

        def cleared(b, tag=None):
            page = tile([P, T], F32, "page%d" % b, tag)
            nc.vector.memset(page[:].bitcast(I32), 0)
            return page

        def places_of(page, first, last):
            return page[:].indirect(places[:, first // PER_COLUMN : last // PER_COLUMN])

        half = I // 2
        pages = [cleared(0), cleared(1), cleared(2, "x1")]

        at0 = quantised(0)
        for h in range(2):
            bank = mixed(at0, h * half, (h + 1) * half, "bank%d" % (2 + h))
            m = tile([P, half], F32, "m0_%d" % h)
            nc.scalar.copy(m[:], bank[:])
            nc.scalar.activation(places_of(pages[0], h * half, (h + 1) * half), m[:], COPY)

        bank1 = mixed(quantised(1), 0, I, "bank4")
        pages.append(cleared(3, "at1"))
        bank2 = mixed(quantised(2), 0, I, "bank5")
        m = tile([P, SHARE], F32, "m1_first")
        nc.vector.tensor_copy(m[:], bank1[:, 0:SHARE])
        nc.vector.tensor_copy(places_of(pages[1], 0, SHARE), m[:])
        bank3 = mixed(quantised(3), 0, I, "bank6")
        m = tile([P, I - SHARE], F32, "m1_rest", "at3")
        nc.vector.tensor_copy(m[:], bank1[:, SHARE:I])
        nc.vector.tensor_copy(places_of(pages[1], SHARE, I), m[:])

        m = tile([P, I], F32, "m2")
        nc.scalar.copy(m[:], bank2[:])
        nc.scalar.activation(places_of(pages[2], 0, I - SHARE), m[:, 0 : I - SHARE], COPY)
        nc.vector.tensor_copy(places_of(pages[2], I - SHARE, I), m[:, I - SHARE : I])

        m = tile([P, I], F32, "m3")
        nc.scalar.copy(m[:], bank3[:])
        for h in range(2):
            nc.scalar.activation(places_of(pages[3], h * half, (h + 1) * half), m[:, h * half : (h + 1) * half], COPY)

        res_tags = ["x0", "got0", "got1", "w_words"]
        rows = []
        for b in range(TILES):
            row = tile([P, T], F32, "res%d" % b, res_tags[b])
            nc.sync.dma_start(out=row[:], in_=res[P * b : P * (b + 1), :])
            rows.append(row)

        for b in range(TILES):
            result = tile([P, T], F32, "result%d" % b, "at3" if b == 0 else None)
            parts = 2 if b == TILES - 1 else 1
            width = T // parts
            for h in range(parts):
                cols = slice(h * width, (h + 1) * width)
                nc.vector.scalar_tensor_tensor(
                    result[:, cols], rows[b][:, cols], RES_FACTOR, pages[b][:, cols], MULT, ADD
                )
                nc.sync.dma_start(out=out[P * b : P * (b + 1), cols], in_=result[:, cols])
